import numpy as np
import ml_dtypes


def mxq(x, axis, fmt="e4m3"):
    dtype, down = {"e4m3": (ml_dtypes.float8_e4m3fn, 7), "e5m2": (ml_dtypes.float8_e5m2, 14)}[fmt]
    v = np.moveaxis(np.asarray(x, np.float32).astype(ml_dtypes.bfloat16).astype(np.float64), axis, -1)
    blocks = v.reshape(v.shape[:-1] + (-1, 32))
    amax = np.abs(blocks).max(-1, keepdims=True)
    byte = np.maximum(np.where(amax > 0, np.frexp(amax)[1] - 1 + 127, 0) - down, 1)
    scale = np.exp2(byte - 127.0)
    codes = (blocks / scale).astype(np.float32).astype(dtype).astype(np.float64)
    return np.moveaxis((codes * scale).reshape(v.shape), -1, axis)


WIDE = False


def mx_kscale(k):
    if not WIDE:
        return np.ones(k)
    levels = np.array([10, -10, 5, -5, 0])
    if k % 512:
        return np.exp2(np.random.permutation(np.resize(levels, k // 32))).repeat(32)
    a = np.empty((k // 512, 16))
    for p in range(k // 512):
        a[p, :8] = np.random.permutation(np.resize(levels, 8))
        for g in range(8):
            far = levels[np.abs(levels - a[p, g]) >= 10]
            a[p, g + 8] = far[np.random.randint(len(far))]
    return np.exp2(a.ravel()).repeat(32)


def f64(x):
    return np.asarray(x).astype(np.float64)


def striped(idx):
    return np.tile(idx.reshape(-1, 16).T, (8, 1)).astype(np.uint16)


def unstriped(offs):
    return offs[:16].T.reshape(-1).astype(np.int64)


def pack_weight(w):
    k, n = w.shape
    w = f64(np.asarray(w, np.float32).astype(ml_dtypes.bfloat16)).reshape(k // 32, 32, n)
    amax = np.abs(w).max(1)
    byte = np.clip(np.where(amax > 0, np.frexp(amax)[1] - 1 + 127 - 7, 1), 1, 254)
    scaled = (w * np.exp2(127.0 - byte)[:, None, :]).reshape(k, n).astype(np.float32)
    words = np.ascontiguousarray(scaled.reshape(k // 512, 128, 4, n).transpose(0, 1, 3, 2)).astype(ml_dtypes.float8_e4m3fn).view(np.uint8)
    return words, np.ascontiguousarray(byte.astype(np.uint8).reshape(k // 512, 16, n))


def unpack_weight(words, scales):
    g, p, n, _ = words.shape
    vals = np.ascontiguousarray(words).view(ml_dtypes.float8_e4m3fn).astype(np.float64) * np.repeat(np.exp2(scales.astype(np.float64) - 127.0), 8, axis=1)[..., None]
    return vals.transpose(0, 1, 3, 2).reshape(g * 512, n)


K, T, S, H, N = 1024, 1024, 512, 512, 128


def setup_inputs():
    n = np.random.standard_normal
    s = mx_kscale(K)[:, None]
    u = mx_kscale(H)
    packed_xT = pack_weight(n((K, T)) * s)
    return {
        "x_words": packed_xT[0],
        "x_scales": packed_xT[1],
        "w1": (n((K, H)) / np.sqrt(K) / s).astype(np.float32),
        "unit": (np.random.uniform(0.5, 1.5, (H, 1)) * u[:, None]).astype(np.float32),
        "wx": (n((H, 1))).astype(np.float32),
        "wt": (n((H, 1))).astype(np.float32),
        "w2": (n((H, N)) / np.sqrt(H) / u[:, None]).astype(np.float32),
        "offs": striped(np.random.permutation(T)[:S]),
    }


def reference(x_words, x_scales, w1, unit, wx, wt, w2, offs):
    xq = unpack_weight(x_words, x_scales)[:, unstriped(offs)]
    h = np.tanh(mxq(f64(w1), 0, "e4m3").T @ xq)
    h1 = -1.0 * ((h) ** 2) + 1.0
    zut = f64(unit) * (f64(wt) * h1)
    w2q = mxq(f64(w2), 0, "e4m3")
    ut = w2q.T @ mxq(zut, 0, "e4m3")
    zuxx = f64(unit) * (f64(wx) * (f64(wx) * (-2.0 * (h * h1))))
    uxx = w2q.T @ mxq(zuxx, 0, "e4m3")
    zu0 = f64(unit) * h
    u0 = w2q.T @ mxq(zu0, 0, "e4m3")
    return ut - (0.5 * uxx) - u0 + u0 * ((u0) ** 2)

@@ -1,0 +1,219 @@
+from contextlib import ExitStack
+
+import concourse.mybir as mybir
+
+K, T, S, H, N = 1024, 1024, 512, 512, 128
+FLOPS = 2 * K * H * S + 3 * 2 * H * N * S
+
+F32 = mybir.dt.float32
+BF16 = mybir.dt.bfloat16
+I32 = mybir.dt.int32
+U32 = mybir.dt.uint32
+U16 = mybir.dt.uint16
+U8 = mybir.dt.uint8
+FP8X4 = mybir.dt.float8_e4m3fn_x4
+ACT = mybir.ActivationFunctionType
+ALU = mybir.AluOpType
+
+P = 128
+PACK = 4
+PASSES = K // (P * PACK)
+CHUNKS = [(0, 128, False), (128, 256, True), (384, 128, False)]
+
+
+def tile_picked_ypinn_allen_p_kernel(
+    tc, x_words, x_scales, w1, unit, wx, wt, w2, offs, out
+):
+    nc = tc.nc
+    with ExitStack() as ctx:
+        sb = ctx.enter_context(tc.tile_pool(name="sb", bufs=1))
+        ps = ctx.enter_context(tc.psum_pool(name="ps", bufs=1))
+
+        def tile(name, shape, dtype):
+            return sb.tile(shape, dtype, name=name, align_bytes=64)
+
+        def bank(name, tag, shape):
+            return ps.tile(shape, F32, name=name, tag=tag)
+
+        offsets = tile("offsets", [P, S // 16], U16)
+        xw = [tile("xw%d" % g, [P, T], U32) for g in range(PASSES)]
+        xs = tile("xs", [P, T], U8)
+        w1raw = [tile("w1raw%d" % g, [P, PACK, H], F32) for g in range(PASSES)]
+        w2raw = tile("w2raw", [P, PACK, N], F32)
+        unit_sb = tile("unit_sb", [P, PACK], F32)
+        wx_sb = tile("wx_sb", [P, PACK], F32)
+        wt_sb = tile("wt_sb", [P, PACK], F32)
+        warm = tile("warm", [P, 2], F32)
+
+        nc.gpsimd.memset(xs[:].bitcast(I32), 0)
+        nc.gpsimd.memset(warm[:, 0:1], 0.0)
+        nc.scalar.activation(out=warm[:, 1:2], in_=warm[:, 0:1], func=ACT.Tanh)
+
+        def load_words(g):
+            nc.sync.dma_start(
+                out=xw[g][:].bitcast(I32),
+                in_=x_words[g].rearrange("p n t -> p (n t)").bitcast(I32),
+            )
+
+        def load_w1(g):
+            rows = w1[g * P * PACK : (g + 1) * P * PACK, :]
+            nc.sync.dma_start(out=w1raw[g][:], in_=rows.rearrange("(p j) c -> p j c", j=PACK))
+
+        load_words(0)
+        nc.sync.dma_start(offsets[:], offs)
+        for q in range(4):
+            nc.sync.dma_start(
+                out=xs[32 * q : 32 * q + 4 * PASSES, :].bitcast(I32),
+                in_=x_scales[:, 4 * q : 4 * q + 4, :].bitcast(I32),
+            )
+        load_w1(0)
+        load_w1(1)
+        load_words(1)
+        nc.sync.dma_start(out=w2raw[:], in_=w2.rearrange("(p j) n -> p j n", j=PACK))
+        for dst, src in ((wx_sb, wx), (unit_sb, unit), (wt_sb, wt)):
+            nc.gpsimd.dma_start(out=dst[:], in_=src.rearrange("(p j) o -> p (j o)", j=PACK))
+
+        gs = tile("gs", [P, S], U8)
+        g0 = tile("g0", [P, S], U32)
+        nc.vector.tensor_copy(out=g0[:], in_=xw[0][:].indirect(offsets[:]))
+        nc.vector.tensor_copy(out=gs[:], in_=xs[:].indirect(offsets[:]))
+
+        coef = tile("coef", [P, 5, PACK], F32)
+        a_pos, a_neg, c_pos, c_neg, wx2 = [coef[:, i, :] for i in range(5)]
+        nc.gpsimd.tensor_tensor(out=wx2, in0=wx_sb[:], in1=wx_sb[:], op=ALU.mult)
+        nc.gpsimd.tensor_tensor(out=c_pos, in0=unit_sb[:], in1=wx2, op=ALU.mult)
+        nc.gpsimd.tensor_scalar(out=c_neg, in0=c_pos, scalar1=-1.0, scalar2=0.0, op0=ALU.mult, op1=ALU.add)
+        nc.gpsimd.tensor_tensor(out=a_pos, in0=unit_sb[:], in1=wt_sb[:], op=ALU.mult)
+        nc.gpsimd.tensor_scalar(out=a_neg, in0=a_pos, scalar1=-1.0, scalar2=0.0, op0=ALU.mult, op1=ALU.add)
+
+        w1q, w1s = {}, {}
+        for g in range(PASSES):
+            src = w1raw[g][:].rearrange("p j (m t) -> p m j t", t=PACK)
+            bf = [tile("w1bf%d%d" % (g, u), [P, 2, P, PACK], BF16) for u in range(2)]
+            nc.vector.tensor_copy(out=bf[0][:].rearrange("p t m j -> p m j t"), in_=src[:, :, :, 0:2])
+            nc.scalar.copy(out=bf[1][:].rearrange("p t m j -> p m j t"), in_=src[:, :, :, 2:4])
+            for u in range(2):
+                words = tile("w1q%d%d" % (g, u), [P, 2 * P], U32)
+                scales = tile("w1s%d%d" % (g, u), [P, 2 * P], U8)
+                nc.vector.quantize_mx(out=words[:].bitcast(FP8X4), scales=scales[:], in_=bf[u][:].rearrange("p t m j -> p (t m j)"))
+                for v in range(2):
+                    w1q[g, 2 * u + v] = words[:, v * P : (v + 1) * P]
+                    w1s[g, 2 * u + v] = scales[:, v * P : (v + 1) * P]
+
+        g1 = []
+        for ci, (c0, n, on_scalar) in enumerate(CHUNKS):
+            g1.append(tile("g1_%d" % ci, [P, n], U32))
+
+        def gather1(ci):
+            c0, n, on_scalar = CHUNKS[ci]
+            nc.vector.tensor_copy(out=g1[ci][:], in_=xw[1][:].indirect(offsets[:, c0 // 16 : (c0 + n) // 16]))
+
+        def mm1(dst, ci, g, t):
+            c0, n, on_scalar = CHUNKS[ci]
+            rhs = g0[:, c0 : c0 + n] if g == 0 else g1[ci][:]
+            nc.tensor.matmul_mx(
+                out=dst,
+                lhsT=w1q[g, t].bitcast(FP8X4),
+                lhsT_scale=w1s[g, t],
+                rhs=rhs.bitcast(FP8X4),
+                rhs_scale=gs[4 * g : P, c0 : c0 + n],
+                start=(g == 0),
+                stop=(g == PASSES - 1),
+            )
+
+        hs = [tile("h%d" % ci, [P, PACK, c[1]], F32) for ci, c in enumerate(CHUNKS)]
+
+        def first_layer(ci, tags):
+            c0, n, on_scalar = CHUNKS[ci]
+            per = PACK // len(tags)
+            banks = [bank("z%d_%d" % (ci, b), tags[b], [P, per, n]) for b in range(len(tags))]
+            if per == 1:
+                for g in range(PASSES):
+                    for t in range(PACK):
+                        mm1(banks[t][:, 0, :], ci, g, t)
+            else:
+                for t in range(PACK):
+                    for g in range(PASSES):
+                        mm1(banks[t // per][:, t % per, :], ci, g, t)
+            return banks
+
+        def tanh(ci, banks):
+            per = PACK // len(banks)
+            for b in range(len(banks)):
+                nc.scalar.activation(out=hs[ci][:, b * per : (b + 1) * per, :], in_=banks[b][:], func=ACT.Tanh)
+
+        gather1(0)
+        banks0 = first_layer(0, ["b0", "b1", "b2", "b3"])
+        gather1(1)
+        banks1 = first_layer(1, ["b4", "b5"])
+        gather1(2)
+        banks2 = first_layer(2, ["b6"])
+        zbanks = [banks0, banks1, banks2]
+
+        w2bf = tile("w2bf", [P, N, PACK], BF16)
+        w2q = tile("w2q", [P, N], U32)
+        w2s = tile("w2s", [P, N], U8)
+        nc.vector.tensor_copy(
+            out=w2bf[:].rearrange("p (c i) j -> p c j i", i=4),
+            in_=w2raw[:].rearrange("p j (c i) -> p c j i", i=4),
+        )
+        nc.vector.quantize_mx(out=w2q[:].bitcast(FP8X4), scales=w2s[:], in_=w2bf[:].rearrange("p n j -> p (n j)"))
+
+        def quantised_product(name, z, n, dst, start, stop):
+            words = tile(name + "q", [P, n], U32)
+            scales = tile(name + "s", [P, n], U8)
+            nc.vector.quantize_mx(out=words[:].bitcast(FP8X4), scales=scales[:], in_=z[:].rearrange("p n t -> p (n t)"))
+            nc.tensor.matmul_mx(
+                out=dst, lhsT=w2q[:].bitcast(FP8X4), lhsT_scale=w2s[:],
+                rhs=words[:].bitcast(FP8X4), rhs_scale=scales[:], start=start, stop=stop,
+            )
+
+        def walk_src(x):
+            return x[:].rearrange("p t (c i) -> p c t i", i=4)
+
+        def walk_dst(z):
+            return z[:].rearrange("p (c i) t -> p c t i", i=4)
+
+        out_tags = [("b0", "b1"), ("b2", "b3"), ("b7", "b4")]
+        for ci, (c0, n, on_scalar) in enumerate(CHUNKS):
+            tanh(ci, zbanks[ci])
+            h = hs[ci]
+            sq = tile("sq%d" % ci, [P, PACK, n], F32)
+            mc = tile("mc%d" % ci, [P, PACK, n], F32)
+            zu0 = tile("zu0_%d" % ci, [P, n, PACK], BF16)
+            zut = tile("zut_%d" % ci, [P, n, PACK], BF16)
+            zxx = tile("zxx_%d" % ci, [P, n, PACK], BF16)
+            u0 = bank("u0_%d" % ci, out_tags[ci][0], [P, n])
+            lin = bank("lin_%d" % ci, out_tags[ci][1], [P, n])
+            nc.scalar.activation(out=sq[:], in_=h[:], func=ACT.Square)
+            for t in range(PACK):
+                nc.scalar.activation(out=mc[:, t, :], in_=sq[:, t, :], func=ACT.Identity, scale=c_neg[:, t : t + 1], bias=c_pos[:, t : t + 1])
+            nc.vector.tensor_tensor(
+                out=walk_dst(zu0), in0=walk_src(h),
+                in1=unit_sb[:].unsqueeze(1).unsqueeze(3).to_broadcast([P, n // 4, PACK, 4]), op=ALU.mult,
+            )
+            if on_scalar:
+                ma = tile("ma%d" % ci, [P, PACK, n], F32)
+                for t in range(PACK):
+                    nc.scalar.activation(out=ma[:, t, :], in_=sq[:, t, :], func=ACT.Identity, scale=a_neg[:, t : t + 1], bias=a_pos[:, t : t + 1])
+                nc.vector.tensor_tensor(out=walk_dst(zxx), in0=walk_src(mc), in1=walk_src(h), op=ALU.mult)
+                quantised_product("zu0_%d" % ci, zu0, n, u0[:], True, True)
+                nc.vector.tensor_copy(out=walk_dst(zut), in_=walk_src(ma))
+                quantised_product("zxx_%d" % ci, zxx, n, lin[:], True, False)
+                quantised_product("zut_%d" % ci, zut, n, lin[:], False, True)
+            else:
+                nc.vector.scalar_tensor_tensor(
+                    out=zut[:], in0=sq[:].rearrange("p t n -> p n t"), scalar=1.0,
+                    in1=a_neg.unsqueeze(1).to_broadcast([P, n, PACK]), op0=ALU.subtract, op1=ALU.mult,
+                )
+                quantised_product("zu0_%d" % ci, zu0, n, u0[:], True, True)
+                nc.vector.tensor_tensor(out=walk_dst(zxx), in0=walk_src(mc), in1=walk_src(h), op=ALU.mult)
+                quantised_product("zut_%d" % ci, zut, n, lin[:], True, False)
+                quantised_product("zxx_%d" % ci, zxx, n, lin[:], False, True)
+            usq = tile("usq%d" % ci, [P, n], F32)
+            cub = tile("cub%d" % ci, [P, n], F32)
+            res = tile("res%d" % ci, [P, n], F32)
+            nc.scalar.activation(out=usq[:], in_=u0[:], func=ACT.Square)
+            nc.vector.scalar_tensor_tensor(out=cub[:], in0=usq[:], scalar=1.0, in1=u0[:], op0=ALU.subtract, op1=ALU.mult)
+            nc.vector.tensor_tensor(out=res[:], in0=cub[:], in1=lin[:], op=ALU.add)
+            nc.sync.dma_start(out=out[:, c0 : c0 + n], in_=res[:])

@@ -18,7 +18,10 @@ ALU = mybir.AluOpType
 P = 128
 PACK = 4
 PASSES = K // (P * PACK)
-CHUNKS = [(0, 128, False), (128, 256, True), (384, 128, False)]
+M_SPLIT = 96
+M_LAST = 48
+COEF_TAG = "xs"
+CHUNKS = [(0, 128, False), (128, 256, True), (384, 128, True)]
 
 
 def tile_picked_ypinn_allen_p_kernel(
@@ -29,8 +32,8 @@ def tile_picked_ypinn_allen_p_kernel(
         sb = ctx.enter_context(tc.tile_pool(name="sb", bufs=1))
         ps = ctx.enter_context(tc.psum_pool(name="ps", bufs=1))
 
-        def tile(name, shape, dtype):
-            return sb.tile(shape, dtype, name=name, align_bytes=64)
+        def tile(name, shape, dtype, tag=""):
+            return sb.tile(shape, dtype, name=name, tag=tag or name, align_bytes=64)
 
         def bank(name, tag, shape):
             return ps.tile(shape, F32, name=name, tag=tag)
@@ -38,7 +41,8 @@ def tile_picked_ypinn_allen_p_kernel(
         offsets = tile("offsets", [P, S // 16], U16)
         xw = [tile("xw%d" % g, [P, T], U32) for g in range(PASSES)]
         xs = tile("xs", [P, T], U8)
-        w1raw = [tile("w1raw%d" % g, [P, PACK, H], F32) for g in range(PASSES)]
+        w1raw = [tile("w1raw%d" % g, [P, PACK, H], F32) for g in range(1)]
+        w1half = [tile("w1half%d" % u, [P, PACK, 256], F32) for u in range(2)]
         w2raw = tile("w2raw", [P, PACK, N], F32)
         unit_sb = tile("unit_sb", [P, PACK], F32)
         wx_sb = tile("wx_sb", [P, PACK], F32)
@@ -67,35 +71,43 @@ def tile_picked_ypinn_allen_p_kernel(
                 in_=x_scales[:, 4 * q : 4 * q + 4, :].bitcast(I32),
             )
         load_w1(0)
-        load_w1(1)
+        for u in range(2):
+            rows = w1[P * PACK :, u * 256 : (u + 1) * 256]
+            nc.sync.dma_start(out=w1half[u][:], in_=rows.rearrange("(p j) c -> p j c", j=PACK))
         load_words(1)
-        nc.sync.dma_start(out=w2raw[:], in_=w2.rearrange("(p j) n -> p j n", j=PACK))
         for dst, src in ((wx_sb, wx), (unit_sb, unit), (wt_sb, wt)):
             nc.gpsimd.dma_start(out=dst[:], in_=src.rearrange("(p j) o -> p (j o)", j=PACK))
+        nc.sync.dma_start(out=w2raw[:], in_=w2.rearrange("(p j) n -> p j n", j=PACK))
 
         gs = tile("gs", [P, S], U8)
         g0 = tile("g0", [P, S], U32)
         nc.vector.tensor_copy(out=g0[:], in_=xw[0][:].indirect(offsets[:]))
         nc.vector.tensor_copy(out=gs[:], in_=xs[:].indirect(offsets[:]))
 
-        coef = tile("coef", [P, 5, PACK], F32)
-        a_pos, a_neg, c_pos, c_neg, wx2 = [coef[:, i, :] for i in range(5)]
-        nc.gpsimd.tensor_tensor(out=wx2, in0=wx_sb[:], in1=wx_sb[:], op=ALU.mult)
-        nc.gpsimd.tensor_tensor(out=c_pos, in0=unit_sb[:], in1=wx2, op=ALU.mult)
-        nc.gpsimd.tensor_scalar(out=c_neg, in0=c_pos, scalar1=-1.0, scalar2=0.0, op0=ALU.mult, op1=ALU.add)
-        nc.gpsimd.tensor_tensor(out=a_pos, in0=unit_sb[:], in1=wt_sb[:], op=ALU.mult)
-        nc.gpsimd.tensor_scalar(out=a_neg, in0=a_pos, scalar1=-1.0, scalar2=0.0, op0=ALU.mult, op1=ALU.add)
+        coef = tile("coef", [P, 5, PACK], F32, tag=COEF_TAG)
+        a_pos, c_pos, a_neg, c_neg, wx2 = [coef[:, i, :] for i in range(5)]
+        nc.vector.tensor_tensor(out=wx2, in0=wx_sb[:], in1=wx_sb[:], op=ALU.mult)
+        nc.vector.tensor_tensor(out=a_pos, in0=unit_sb[:], in1=wt_sb[:], op=ALU.mult)
+        nc.vector.tensor_tensor(out=c_pos, in0=unit_sb[:], in1=wx2, op=ALU.mult)
+        nc.vector.tensor_scalar(out=coef[:, 2:4, :], in0=coef[:, 0:2, :], scalar1=-1.0, scalar2=None, op0=ALU.mult)
 
         w1q, w1s = {}, {}
         for g in range(PASSES):
-            src = w1raw[g][:].rearrange("p j (m t) -> p m j t", t=PACK)
-            bf = [tile("w1bf%d%d" % (g, u), [P, 2, P, PACK], BF16) for u in range(2)]
-            nc.vector.tensor_copy(out=bf[0][:].rearrange("p t m j -> p m j t"), in_=src[:, :, :, 0:2])
-            nc.scalar.copy(out=bf[1][:].rearrange("p t m j -> p m j t"), in_=src[:, :, :, 2:4])
+            bf = tile("w1bf%d" % g, [P, PACK, P, PACK], BF16)
+            dst = bf[:].rearrange("p t m j -> p m j t")
+            if g == 0:
+                src = w1raw[g][:].rearrange("p j (m t) -> p m j t", t=PACK)
+                nc.vector.tensor_copy(out=dst[:, :M_SPLIT], in_=src[:, :M_SPLIT])
+                nc.scalar.copy(out=dst[:, M_SPLIT:], in_=src[:, M_SPLIT:])
+            else:
+                src = [w1half[u][:].rearrange("p j (m t) -> p m j t", t=PACK) for u in range(2)]
+                nc.scalar.copy(out=dst[:, :64], in_=src[0])
+                nc.vector.tensor_copy(out=dst[:, 64 : 64 + M_LAST], in_=src[1][:, :M_LAST])
+                nc.scalar.copy(out=dst[:, 64 + M_LAST :], in_=src[1][:, M_LAST:])
             for u in range(2):
                 words = tile("w1q%d%d" % (g, u), [P, 2 * P], U32)
                 scales = tile("w1s%d%d" % (g, u), [P, 2 * P], U8)
-                nc.vector.quantize_mx(out=words[:].bitcast(FP8X4), scales=scales[:], in_=bf[u][:].rearrange("p t m j -> p (t m j)"))
+                nc.vector.quantize_mx(out=words[:].bitcast(FP8X4), scales=scales[:], in_=bf[:, 2 * u : 2 * u + 2].rearrange("p t m j -> p (t m j)"))
                 for v in range(2):
                     w1q[g, 2 * u + v] = words[:, v * P : (v + 1) * P]
                     w1s[g, 2 * u + v] = scales[:, v * P : (v + 1) * P]
@@ -159,57 +171,33 @@ def tile_picked_ypinn_allen_p_kernel(
         )
         nc.vector.quantize_mx(out=w2q[:].bitcast(FP8X4), scales=w2s[:], in_=w2bf[:].rearrange("p n j -> p (n j)"))
 
-        def quantised_product(name, z, n, dst, start, stop):
+        def quantise(name, z, n):
             words = tile(name + "q", [P, n], U32)
             scales = tile(name + "s", [P, n], U8)
-            nc.vector.quantize_mx(out=words[:].bitcast(FP8X4), scales=scales[:], in_=z[:].rearrange("p n t -> p (n t)"))
+            nc.vector.quantize_mx(out=words[:].bitcast(FP8X4), scales=scales[:], in_=z)
+            return words, scales
+
+        def mm2(dst, words, scales, start, stop):
             nc.tensor.matmul_mx(
                 out=dst, lhsT=w2q[:].bitcast(FP8X4), lhsT_scale=w2s[:],
-                rhs=words[:].bitcast(FP8X4), rhs_scale=scales[:], start=start, stop=stop,
+                rhs=words.bitcast(FP8X4), rhs_scale=scales, start=start, stop=stop,
             )
 
         def walk_src(x):
             return x[:].rearrange("p t (c i) -> p c t i", i=4)
 
         def walk_dst(z):
-            return z[:].rearrange("p (c i) t -> p c t i", i=4)
+            return z.rearrange("p (c i) t -> p c t i", i=4)
 
-        out_tags = [("b0", "b1"), ("b2", "b3"), ("b7", "b4")]
-        for ci, (c0, n, on_scalar) in enumerate(CHUNKS):
-            tanh(ci, zbanks[ci])
-            h = hs[ci]
-            sq = tile("sq%d" % ci, [P, PACK, n], F32)
-            mc = tile("mc%d" % ci, [P, PACK, n], F32)
-            zu0 = tile("zu0_%d" % ci, [P, n, PACK], BF16)
-            zut = tile("zut_%d" % ci, [P, n, PACK], BF16)
-            zxx = tile("zxx_%d" % ci, [P, n, PACK], BF16)
-            u0 = bank("u0_%d" % ci, out_tags[ci][0], [P, n])
-            lin = bank("lin_%d" % ci, out_tags[ci][1], [P, n])
-            nc.scalar.activation(out=sq[:], in_=h[:], func=ACT.Square)
+        def affine(dst, src, neg, pos, on_scalar):
             for t in range(PACK):
-                nc.scalar.activation(out=mc[:, t, :], in_=sq[:, t, :], func=ACT.Identity, scale=c_neg[:, t : t + 1], bias=c_pos[:, t : t + 1])
-            nc.vector.tensor_tensor(
-                out=walk_dst(zu0), in0=walk_src(h),
-                in1=unit_sb[:].unsqueeze(1).unsqueeze(3).to_broadcast([P, n // 4, PACK, 4]), op=ALU.mult,
-            )
-            if on_scalar:
-                ma = tile("ma%d" % ci, [P, PACK, n], F32)
-                for t in range(PACK):
-                    nc.scalar.activation(out=ma[:, t, :], in_=sq[:, t, :], func=ACT.Identity, scale=a_neg[:, t : t + 1], bias=a_pos[:, t : t + 1])
-                nc.vector.tensor_tensor(out=walk_dst(zxx), in0=walk_src(mc), in1=walk_src(h), op=ALU.mult)
-                quantised_product("zu0_%d" % ci, zu0, n, u0[:], True, True)
-                nc.vector.tensor_copy(out=walk_dst(zut), in_=walk_src(ma))
-                quantised_product("zxx_%d" % ci, zxx, n, lin[:], True, False)
-                quantised_product("zut_%d" % ci, zut, n, lin[:], False, True)
-            else:
-                nc.vector.scalar_tensor_tensor(
-                    out=zut[:], in0=sq[:].rearrange("p t n -> p n t"), scalar=1.0,
-                    in1=a_neg.unsqueeze(1).to_broadcast([P, n, PACK]), op0=ALU.subtract, op1=ALU.mult,
-                )
-                quantised_product("zu0_%d" % ci, zu0, n, u0[:], True, True)
-                nc.vector.tensor_tensor(out=walk_dst(zxx), in0=walk_src(mc), in1=walk_src(h), op=ALU.mult)
-                quantised_product("zut_%d" % ci, zut, n, lin[:], True, False)
-                quantised_product("zxx_%d" % ci, zxx, n, lin[:], False, True)
+                if on_scalar:
+                    nc.scalar.activation(out=dst[:, t, :], in_=src[:, t, :], func=ACT.Identity, scale=neg[:, t : t + 1], bias=pos[:, t : t + 1])
+                else:
+                    nc.vector.tensor_scalar(out=dst[:, t, :], in0=src[:, t, :], scalar1=neg[:, t : t + 1], scalar2=pos[:, t : t + 1], op0=ALU.mult, op1=ALU.add)
+
+        def residual(ci, u0, lin):
+            c0, n, on_scalar = CHUNKS[ci]
             usq = tile("usq%d" % ci, [P, n], F32)
             cub = tile("cub%d" % ci, [P, n], F32)
             res = tile("res%d" % ci, [P, n], F32)
@@ -217,3 +205,39 @@ def tile_picked_ypinn_allen_p_kernel(
             nc.vector.scalar_tensor_tensor(out=cub[:], in0=usq[:], scalar=1.0, in1=u0[:], op0=ALU.subtract, op1=ALU.mult)
             nc.vector.tensor_tensor(out=res[:], in0=cub[:], in1=lin[:], op=ALU.add)
             nc.sync.dma_start(out=out[:, c0 : c0 + n], in_=res[:])
+
+        out_tags = [("b0", "b1"), ("b2", "b3"), ("b7", "b4")]
+        sums = []
+        for ci, (c0, n, on_scalar) in enumerate(CHUNKS):
+            tanh(ci, zbanks[ci])
+            h = hs[ci]
+            sq = tile("sq%d" % ci, [P, PACK, n], F32)
+            mc = tile("mc%d" % ci, [P, PACK, n], F32)
+            ma = tile("ma%d" % ci, [P, PACK, n], F32)
+            zu0 = tile("zu0_%d" % ci, [P, n, PACK], BF16)
+            zd = tile("zd_%d" % ci, [P, 2, n, PACK], BF16)
+            u0 = bank("u0_%d" % ci, out_tags[ci][0], [P, n])
+            lin = bank("lin_%d" % ci, out_tags[ci][1], [P, n])
+            nc.scalar.activation(out=sq[:], in_=h[:], func=ACT.Square)
+            affine(mc, sq, c_neg, c_pos, on_scalar)
+            nc.vector.tensor_tensor(
+                out=walk_dst(zu0[:]), in0=walk_src(h),
+                in1=unit_sb[:].unsqueeze(1).unsqueeze(3).to_broadcast([P, n // 4, PACK, 4]), op=ALU.mult,
+            )
+            affine(ma, sq, a_neg, a_pos, on_scalar)
+            words, scales = quantise("zu0_%d" % ci, zu0[:].rearrange("p n t -> p (n t)"), n)
+            mm2(u0[:], words[:], scales[:], True, True)
+            nc.vector.tensor_tensor(out=walk_dst(zd[:, 0]), in0=walk_src(mc), in1=walk_src(h), op=ALU.mult)
+            nc.vector.tensor_copy(out=walk_dst(zd[:, 1]), in_=walk_src(ma))
+            if ci < len(CHUNKS) - 1:
+                words, scales = quantise("zd_%d" % ci, zd[:].rearrange("p a n t -> p (a n t)"), 2 * n)
+                for a in range(2):
+                    mm2(lin[:], words[:, a * n : (a + 1) * n], scales[:, a * n : (a + 1) * n], a == 0, a == 1)
+            else:
+                for a in range(2):
+                    words, scales = quantise("zd_%d%d" % (ci, a), zd[:, a].rearrange("p n t -> p (n t)"), n)
+                    mm2(lin[:], words[:], scales[:], a == 0, a == 1)
+            sums.append((u0, lin))
+            if ci > 0:
+                residual(ci - 1, *sums[ci - 1])
+        residual(len(CHUNKS) - 1, *sums[-1])

@@ -20,7 +20,7 @@ PACK = 4
 PASSES = K // (P * PACK)
 M_SPLIT = 96
 M_LAST = 48
-COEF_TAG = "xs"
+COEF_TAG = "coef"
 CHUNKS = [(0, 128, False), (128, 256, True), (384, 128, True)]
 
 
@@ -46,7 +46,7 @@ def tile_picked_ypinn_allen_p_kernel(
         w2raw = tile("w2raw", [P, PACK, N], F32)
         unit_sb = tile("unit_sb", [P, PACK], F32)
         wx_sb = tile("wx_sb", [P, PACK], F32)
-        wt_sb = tile("wt_sb", [P, PACK], F32)
+        slopes = tile("slopes", [P, 2, PACK], F32)
         warm = tile("warm", [P, 2], F32)
 
         nc.gpsimd.memset(xs[:].bitcast(I32), 0)
@@ -75,21 +75,14 @@ def tile_picked_ypinn_allen_p_kernel(
             rows = w1[P * PACK :, u * 256 : (u + 1) * 256]
             nc.sync.dma_start(out=w1half[u][:], in_=rows.rearrange("(p j) c -> p j c", j=PACK))
         load_words(1)
-        for dst, src in ((wx_sb, wx), (unit_sb, unit), (wt_sb, wt)):
-            nc.gpsimd.dma_start(out=dst[:], in_=src.rearrange("(p j) o -> p (j o)", j=PACK))
+        for dst, src in ((wx_sb[:], wx), (unit_sb[:], unit), (slopes[:, 0, :], wt)):
+            nc.sync.dma_start(out=dst, in_=src.rearrange("(p j) o -> p (j o)", j=PACK))
         nc.sync.dma_start(out=w2raw[:], in_=w2.rearrange("(p j) n -> p j n", j=PACK))
 
         gs = tile("gs", [P, S], U8)
         g0 = tile("g0", [P, S], U32)
         nc.vector.tensor_copy(out=g0[:], in_=xw[0][:].indirect(offsets[:]))
         nc.vector.tensor_copy(out=gs[:], in_=xs[:].indirect(offsets[:]))
-
-        coef = tile("coef", [P, 5, PACK], F32, tag=COEF_TAG)
-        a_pos, c_pos, a_neg, c_neg, wx2 = [coef[:, i, :] for i in range(5)]
-        nc.vector.tensor_tensor(out=wx2, in0=wx_sb[:], in1=wx_sb[:], op=ALU.mult)
-        nc.vector.tensor_tensor(out=a_pos, in0=unit_sb[:], in1=wt_sb[:], op=ALU.mult)
-        nc.vector.tensor_tensor(out=c_pos, in0=unit_sb[:], in1=wx2, op=ALU.mult)
-        nc.vector.tensor_scalar(out=coef[:, 2:4, :], in0=coef[:, 0:2, :], scalar1=-1.0, scalar2=None, op0=ALU.mult)
 
         w1q, w1s = {}, {}
         for g in range(PASSES):
@@ -157,10 +150,18 @@ def tile_picked_ypinn_allen_p_kernel(
         gather1(0)
         banks0 = first_layer(0, ["b0", "b1", "b2", "b3"])
         gather1(1)
-        banks1 = first_layer(1, ["b4", "b5"])
+        banks1 = first_layer(1, ["b4", "b5", "b6", "b7"])
         gather1(2)
-        banks2 = first_layer(2, ["b6"])
+        tanh(0, banks0)
+        banks2 = first_layer(2, ["b3"])
         zbanks = [banks0, banks1, banks2]
+
+        coef = tile("coef", [P, 4, PACK], F32)
+        a_pos, c_pos, a_neg, c_neg = [coef[:, i, :] for i in range(4)]
+        unit2 = unit_sb[:].unsqueeze(1).to_broadcast([P, 2, PACK])
+        nc.vector.tensor_tensor(out=slopes[:, 1, :], in0=wx_sb[:], in1=wx_sb[:], op=ALU.mult)
+        nc.vector.tensor_tensor(out=coef[:, 0:2, :], in0=slopes[:], in1=unit2, op=ALU.mult)
+        nc.vector.scalar_tensor_tensor(out=coef[:, 2:4, :], in0=slopes[:], scalar=-1.0, in1=unit2, op0=ALU.mult, op1=ALU.mult)
 
         w2bf = tile("w2bf", [P, N, PACK], BF16)
         w2q = tile("w2q", [P, N], U32)
@@ -196,28 +197,31 @@ def tile_picked_ypinn_allen_p_kernel(
                 else:
                     nc.vector.tensor_scalar(out=dst[:, t, :], in0=src[:, t, :], scalar1=neg[:, t : t + 1], scalar2=pos[:, t : t + 1], op0=ALU.mult, op1=ALU.add)
 
-        def residual(ci, u0, lin):
-            c0, n, on_scalar = CHUNKS[ci]
+        def residual(ci, c0, n, u0, lin):
             usq = tile("usq%d" % ci, [P, n], F32)
             cub = tile("cub%d" % ci, [P, n], F32)
             res = tile("res%d" % ci, [P, n], F32)
-            nc.scalar.activation(out=usq[:], in_=u0[:], func=ACT.Square)
-            nc.vector.scalar_tensor_tensor(out=cub[:], in0=usq[:], scalar=1.0, in1=u0[:], op0=ALU.subtract, op1=ALU.mult)
-            nc.vector.tensor_tensor(out=res[:], in0=cub[:], in1=lin[:], op=ALU.add)
+            nc.scalar.activation(out=usq[:], in_=u0, func=ACT.Square)
+            nc.vector.scalar_tensor_tensor(out=cub[:], in0=usq[:], scalar=1.0, in1=u0, op0=ALU.subtract, op1=ALU.mult)
+            nc.vector.tensor_tensor(out=res[:], in0=cub[:], in1=lin, op=ALU.add)
             nc.sync.dma_start(out=out[:, c0 : c0 + n], in_=res[:])
 
-        out_tags = [("b0", "b1"), ("b2", "b3"), ("b7", "b4")]
-        sums = []
+        head = CHUNKS[-1][0]
+        u0_head = bank("u0_head", "b0", [P, head])
+        lin_head = bank("lin_head", "b1", [P, head])
+        u0_last = bank("u0_last", "b2", [P, S - head])
+        lin_last = bank("lin_last", "b4", [P, S - head])
         for ci, (c0, n, on_scalar) in enumerate(CHUNKS):
-            tanh(ci, zbanks[ci])
+            if ci > 0:
+                tanh(ci, zbanks[ci])
             h = hs[ci]
             sq = tile("sq%d" % ci, [P, PACK, n], F32)
             mc = tile("mc%d" % ci, [P, PACK, n], F32)
             ma = tile("ma%d" % ci, [P, PACK, n], F32)
             zu0 = tile("zu0_%d" % ci, [P, n, PACK], BF16)
             zd = tile("zd_%d" % ci, [P, 2, n, PACK], BF16)
-            u0 = bank("u0_%d" % ci, out_tags[ci][0], [P, n])
-            lin = bank("lin_%d" % ci, out_tags[ci][1], [P, n])
+            u0 = u0_head[:, c0 : c0 + n] if c0 < head else u0_last[:]
+            lin = lin_head[:, c0 : c0 + n] if c0 < head else lin_last[:]
             nc.scalar.activation(out=sq[:], in_=h[:], func=ACT.Square)
             affine(mc, sq, c_neg, c_pos, on_scalar)
             nc.vector.tensor_tensor(
@@ -226,18 +230,16 @@ def tile_picked_ypinn_allen_p_kernel(
             )
             affine(ma, sq, a_neg, a_pos, on_scalar)
             words, scales = quantise("zu0_%d" % ci, zu0[:].rearrange("p n t -> p (n t)"), n)
-            mm2(u0[:], words[:], scales[:], True, True)
+            mm2(u0, words[:], scales[:], True, True)
             nc.vector.tensor_tensor(out=walk_dst(zd[:, 0]), in0=walk_src(mc), in1=walk_src(h), op=ALU.mult)
             nc.vector.tensor_copy(out=walk_dst(zd[:, 1]), in_=walk_src(ma))
             if ci < len(CHUNKS) - 1:
                 words, scales = quantise("zd_%d" % ci, zd[:].rearrange("p a n t -> p (a n t)"), 2 * n)
                 for a in range(2):
-                    mm2(lin[:], words[:, a * n : (a + 1) * n], scales[:, a * n : (a + 1) * n], a == 0, a == 1)
+                    mm2(lin, words[:, a * n : (a + 1) * n], scales[:, a * n : (a + 1) * n], a == 0, a == 1)
             else:
                 for a in range(2):
                     words, scales = quantise("zd_%d%d" % (ci, a), zd[:, a].rearrange("p n t -> p (n t)"), n)
-                    mm2(lin[:], words[:], scales[:], a == 0, a == 1)
-            sums.append((u0, lin))
-            if ci > 0:
-                residual(ci - 1, *sums[ci - 1])
-        residual(len(CHUNKS) - 1, *sums[-1])
+                    mm2(lin, words[:], scales[:], a == 0, a == 1)
+        residual(0, 0, head, u0_head[:], lin_head[:])
+        residual(1, head, S - head, u0_last[:], lin_last[:])

@@ -17,11 +17,17 @@ ALU = mybir.AluOpType
 
 P = 128
 PACK = 4
-PASSES = K // (P * PACK)
-M_SPLIT = 96
-M_LAST = 48
-COEF_TAG = "coef"
-CHUNKS = [(0, 128, False), (128, 256, True), (384, 128, True)]
+K_PASS = P * PACK
+QUADRANTS, QUADRANT = 4, 32
+LIST_ROWS = 16
+RUN = 4
+HALF = P // 2
+
+M_VECTOR_PASS0 = 96
+M_VECTOR_LAST = 48
+
+CHUNKS = [(0, 128), (128, 256), (384, 128)]
+LAST = len(CHUNKS) - 1
 
 
 def tile_picked_ypinn_allen_p_kernel(
@@ -32,214 +38,224 @@ def tile_picked_ypinn_allen_p_kernel(
         sb = ctx.enter_context(tc.tile_pool(name="sb", bufs=1))
         ps = ctx.enter_context(tc.psum_pool(name="ps", bufs=1))
 
-        def tile(name, shape, dtype, tag=""):
-            return sb.tile(shape, dtype, name=name, tag=tag or name, align_bytes=64)
+        def tile(name, shape, dtype):
+            return sb.tile(shape, dtype, name=name, align_bytes=64)
 
-        def bank(name, tag, shape):
-            return ps.tile(shape, F32, name=name, tag=tag)
+        def bank(name, index, shape):
+            return ps.tile(shape, F32, name=name, tag="bank%d" % index)
 
-        offsets = tile("offsets", [P, S // 16], U16)
-        xw = [tile("xw%d" % g, [P, T], U32) for g in range(PASSES)]
-        xs = tile("xs", [P, T], U8)
-        w1raw = [tile("w1raw%d" % g, [P, PACK, H], F32) for g in range(1)]
-        w1half = [tile("w1half%d" % u, [P, PACK, 256], F32) for u in range(2)]
-        w2raw = tile("w2raw", [P, PACK, N], F32)
+        def quantise(name, values, columns):
+            words = tile(name + "_words", [P, columns], U32)
+            scales = tile(name + "_scales", [P, columns], U8)
+            nc.vector.quantize_mx(out=words[:].bitcast(FP8X4), scales=scales[:], in_=values)
+            return words, scales
+
+        def by_runs(grouped):
+            return grouped.rearrange("p t (c i) -> p c t i", i=RUN)
+
+        def into_words(interleaved):
+            return interleaved.rearrange("p (c i) t -> p c t i", i=RUN)
+
+        offsets = tile("offsets", [P, S // LIST_ROWS], U16)
+        x_word_table = [tile("x_word_table%d" % g, [P, T], U32) for g in range(2)]
+        x_scale_table = tile("x_scale_table", [P, T], U8)
+        w1_pass0 = tile("w1_pass0", [P, PACK, H], F32)
+        w1_pass1 = [tile("w1_pass1_%d" % u, [P, PACK, H // 2], F32) for u in range(2)]
+        w2_raw = tile("w2_raw", [P, PACK, N], F32)
         unit_sb = tile("unit_sb", [P, PACK], F32)
         wx_sb = tile("wx_sb", [P, PACK], F32)
         slopes = tile("slopes", [P, 2, PACK], F32)
-        warm = tile("warm", [P, 2], F32)
-
-        nc.gpsimd.memset(xs[:].bitcast(I32), 0)
-        nc.gpsimd.memset(warm[:, 0:1], 0.0)
-        nc.scalar.activation(out=warm[:, 1:2], in_=warm[:, 0:1], func=ACT.Tanh)
 
         def load_words(g):
             nc.sync.dma_start(
-                out=xw[g][:].bitcast(I32),
+                out=x_word_table[g][:].bitcast(I32),
                 in_=x_words[g].rearrange("p n t -> p (n t)").bitcast(I32),
             )
 
-        def load_w1(g):
-            rows = w1[g * P * PACK : (g + 1) * P * PACK, :]
-            nc.sync.dma_start(out=w1raw[g][:], in_=rows.rearrange("(p j) c -> p j c", j=PACK))
+        def load_rows(dst, rows):
+            nc.sync.dma_start(out=dst, in_=rows.rearrange("(p j) c -> p j c", j=PACK))
 
+        nc.gpsimd.memset(x_scale_table[:].bitcast(I32), 0)
         load_words(0)
         nc.sync.dma_start(offsets[:], offs)
-        for q in range(4):
+        for q in range(QUADRANTS):
             nc.sync.dma_start(
-                out=xs[32 * q : 32 * q + 4 * PASSES, :].bitcast(I32),
+                out=x_scale_table[QUADRANT * q : QUADRANT * q + 8, :].bitcast(I32),
                 in_=x_scales[:, 4 * q : 4 * q + 4, :].bitcast(I32),
             )
-        load_w1(0)
+        load_rows(w1_pass0[:], w1[:K_PASS, :])
         for u in range(2):
-            rows = w1[P * PACK :, u * 256 : (u + 1) * 256]
-            nc.sync.dma_start(out=w1half[u][:], in_=rows.rearrange("(p j) c -> p j c", j=PACK))
+            load_rows(w1_pass1[u][:], w1[K_PASS:, u * (H // 2) : (u + 1) * (H // 2)])
         load_words(1)
-        for dst, src in ((wx_sb[:], wx), (unit_sb[:], unit), (slopes[:, 0, :], wt)):
+        load_rows(w2_raw[:], w2)
+        for dst, src in ((unit_sb[:], unit), (wx_sb[:], wx), (slopes[:, 0, :], wt)):
             nc.sync.dma_start(out=dst, in_=src.rearrange("(p j) o -> p (j o)", j=PACK))
-        nc.sync.dma_start(out=w2raw[:], in_=w2.rearrange("(p j) n -> p j n", j=PACK))
 
-        gs = tile("gs", [P, S], U8)
-        g0 = tile("g0", [P, S], U32)
-        nc.vector.tensor_copy(out=g0[:], in_=xw[0][:].indirect(offsets[:]))
-        nc.vector.tensor_copy(out=gs[:], in_=xs[:].indirect(offsets[:]))
+        picked_scales = tile("picked_scales", [P, S], U8)
+        picked_words0 = tile("picked_words0", [P, S], U32)
+        nc.vector.tensor_copy(out=picked_words0[:], in_=x_word_table[0][:].indirect(offsets[:]))
+        nc.vector.tensor_copy(out=picked_scales[:], in_=x_scale_table[:].indirect(offsets[:]))
 
-        w1q, w1s = {}, {}
-        for g in range(PASSES):
-            bf = tile("w1bf%d" % g, [P, PACK, P, PACK], BF16)
-            dst = bf[:].rearrange("p t m j -> p m j t")
-            if g == 0:
-                src = w1raw[g][:].rearrange("p j (m t) -> p m j t", t=PACK)
-                nc.vector.tensor_copy(out=dst[:, :M_SPLIT], in_=src[:, :M_SPLIT])
-                nc.scalar.copy(out=dst[:, M_SPLIT:], in_=src[:, M_SPLIT:])
-            else:
-                src = [w1half[u][:].rearrange("p j (m t) -> p m j t", t=PACK) for u in range(2)]
-                nc.scalar.copy(out=dst[:, :64], in_=src[0])
-                nc.vector.tensor_copy(out=dst[:, 64 : 64 + M_LAST], in_=src[1][:, :M_LAST])
-                nc.scalar.copy(out=dst[:, 64 + M_LAST :], in_=src[1][:, M_LAST:])
+        w1_words, w1_scales = {}, {}
+
+        def deal(raw):
+            return raw[:].rearrange("p j (m t) -> p m j t", t=PACK)
+
+        def quantise_w1(g, dealt):
             for u in range(2):
-                words = tile("w1q%d%d" % (g, u), [P, 2 * P], U32)
-                scales = tile("w1s%d%d" % (g, u), [P, 2 * P], U8)
-                nc.vector.quantize_mx(out=words[:].bitcast(FP8X4), scales=scales[:], in_=bf[:, 2 * u : 2 * u + 2].rearrange("p t m j -> p (t m j)"))
+                values = dealt[:, 2 * u : 2 * u + 2].rearrange("p t m j -> p (t m j)")
+                words, scales = quantise("w1_%d%d" % (g, u), values, 2 * P)
                 for v in range(2):
-                    w1q[g, 2 * u + v] = words[:, v * P : (v + 1) * P]
-                    w1s[g, 2 * u + v] = scales[:, v * P : (v + 1) * P]
+                    w1_words[g, 2 * u + v] = words[:, v * P : (v + 1) * P]
+                    w1_scales[g, 2 * u + v] = scales[:, v * P : (v + 1) * P]
 
-        g1 = []
-        for ci, (c0, n, on_scalar) in enumerate(CHUNKS):
-            g1.append(tile("g1_%d" % ci, [P, n], U32))
+        dealt0 = tile("w1_dealt0", [P, PACK, P, PACK], BF16)
+        dst0 = dealt0[:].rearrange("p t m j -> p m j t")
+        nc.vector.tensor_copy(out=dst0[:, :M_VECTOR_PASS0], in_=deal(w1_pass0)[:, :M_VECTOR_PASS0])
+        nc.scalar.activation(out=dst0[:, M_VECTOR_PASS0:], in_=deal(w1_pass0)[:, M_VECTOR_PASS0:], func=ACT.Copy)
+        quantise_w1(0, dealt0)
 
-        def gather1(ci):
-            c0, n, on_scalar = CHUNKS[ci]
-            nc.vector.tensor_copy(out=g1[ci][:], in_=xw[1][:].indirect(offsets[:, c0 // 16 : (c0 + n) // 16]))
+        dealt1 = tile("w1_dealt1", [P, PACK, P, PACK], BF16)
+        dst1 = dealt1[:].rearrange("p t m j -> p m j t")
+        split = HALF + M_VECTOR_LAST
+        nc.scalar.activation(out=dst1[:, :HALF], in_=deal(w1_pass1[0]), func=ACT.Copy)
+        nc.vector.tensor_copy(out=dst1[:, HALF:split], in_=deal(w1_pass1[1])[:, :M_VECTOR_LAST])
+        nc.scalar.activation(out=dst1[:, split:], in_=deal(w1_pass1[1])[:, M_VECTOR_LAST:], func=ACT.Copy)
+        quantise_w1(1, dealt1)
 
-        def mm1(dst, ci, g, t):
-            c0, n, on_scalar = CHUNKS[ci]
-            rhs = g0[:, c0 : c0 + n] if g == 0 else g1[ci][:]
+        picked_words1 = [tile("picked_words1_%d" % ci, [P, n], U32) for ci, (c0, n) in enumerate(CHUNKS)]
+        hidden = [tile("hidden%d" % ci, [P, PACK, n], F32) for ci, (c0, n) in enumerate(CHUNKS)]
+
+        def gather_pass1(ci):
+            c0, n = CHUNKS[ci]
+            entries = offsets[:, c0 // LIST_ROWS : (c0 + n) // LIST_ROWS]
+            nc.vector.tensor_copy(out=picked_words1[ci][:], in_=x_word_table[1][:].indirect(entries))
+
+        def first_product(dst, ci, g, t):
+            c0, n = CHUNKS[ci]
+            moving = picked_words0[:, c0 : c0 + n] if g == 0 else picked_words1[ci][:]
             nc.tensor.matmul_mx(
                 out=dst,
-                lhsT=w1q[g, t].bitcast(FP8X4),
-                lhsT_scale=w1s[g, t],
-                rhs=rhs.bitcast(FP8X4),
-                rhs_scale=gs[4 * g : P, c0 : c0 + n],
+                lhsT=w1_words[g, t].bitcast(FP8X4),
+                lhsT_scale=w1_scales[g, t],
+                rhs=moving.bitcast(FP8X4),
+                rhs_scale=picked_scales[4 * g : P, c0 : c0 + n],
                 start=(g == 0),
-                stop=(g == PASSES - 1),
+                stop=(g == 1),
             )
 
-        hs = [tile("h%d" % ci, [P, PACK, c[1]], F32) for ci, c in enumerate(CHUNKS)]
-
-        def first_layer(ci, tags):
-            c0, n, on_scalar = CHUNKS[ci]
-            per = PACK // len(tags)
-            banks = [bank("z%d_%d" % (ci, b), tags[b], [P, per, n]) for b in range(len(tags))]
-            if per == 1:
-                for g in range(PASSES):
-                    for t in range(PACK):
-                        mm1(banks[t][:, 0, :], ci, g, t)
-            else:
+        def first_layer_in_four_banks(ci, first_bank):
+            banks = [bank("pre%d_%d" % (ci, t), first_bank + t, [P, CHUNKS[ci][1]]) for t in range(PACK)]
+            for g in range(2):
                 for t in range(PACK):
-                    for g in range(PASSES):
-                        mm1(banks[t // per][:, t % per, :], ci, g, t)
+                    first_product(banks[t][:], ci, g, t)
             return banks
 
-        def tanh(ci, banks):
-            per = PACK // len(banks)
-            for b in range(len(banks)):
-                nc.scalar.activation(out=hs[ci][:, b * per : (b + 1) * per, :], in_=banks[b][:], func=ACT.Tanh)
-
-        gather1(0)
-        banks0 = first_layer(0, ["b0", "b1", "b2", "b3"])
-        gather1(1)
-        banks1 = first_layer(1, ["b4", "b5", "b6", "b7"])
-        gather1(2)
-        tanh(0, banks0)
-        banks2 = first_layer(2, ["b3"])
-        zbanks = [banks0, banks1, banks2]
-
-        coef = tile("coef", [P, 4, PACK], F32)
-        a_pos, c_pos, a_neg, c_neg = [coef[:, i, :] for i in range(4)]
-        unit2 = unit_sb[:].unsqueeze(1).to_broadcast([P, 2, PACK])
-        nc.vector.tensor_tensor(out=slopes[:, 1, :], in0=wx_sb[:], in1=wx_sb[:], op=ALU.mult)
-        nc.vector.tensor_tensor(out=coef[:, 0:2, :], in0=slopes[:], in1=unit2, op=ALU.mult)
-        nc.vector.scalar_tensor_tensor(out=coef[:, 2:4, :], in0=slopes[:], scalar=-1.0, in1=unit2, op0=ALU.mult, op1=ALU.mult)
-
-        w2bf = tile("w2bf", [P, N, PACK], BF16)
-        w2q = tile("w2q", [P, N], U32)
-        w2s = tile("w2s", [P, N], U8)
-        nc.vector.tensor_copy(
-            out=w2bf[:].rearrange("p (c i) j -> p c j i", i=4),
-            in_=w2raw[:].rearrange("p j (c i) -> p c j i", i=4),
-        )
-        nc.vector.quantize_mx(out=w2q[:].bitcast(FP8X4), scales=w2s[:], in_=w2bf[:].rearrange("p n j -> p (n j)"))
-
-        def quantise(name, z, n):
-            words = tile(name + "q", [P, n], U32)
-            scales = tile(name + "s", [P, n], U8)
-            nc.vector.quantize_mx(out=words[:].bitcast(FP8X4), scales=scales[:], in_=z)
-            return words, scales
-
-        def mm2(dst, words, scales, start, stop):
-            nc.tensor.matmul_mx(
-                out=dst, lhsT=w2q[:].bitcast(FP8X4), lhsT_scale=w2s[:],
-                rhs=words.bitcast(FP8X4), rhs_scale=scales, start=start, stop=stop,
-            )
-
-        def walk_src(x):
-            return x[:].rearrange("p t (c i) -> p c t i", i=4)
-
-        def walk_dst(z):
-            return z.rearrange("p (c i) t -> p c t i", i=4)
-
-        def affine(dst, src, neg, pos, on_scalar):
+        def tanh_of_four_banks(ci, banks):
             for t in range(PACK):
-                if on_scalar:
-                    nc.scalar.activation(out=dst[:, t, :], in_=src[:, t, :], func=ACT.Identity, scale=neg[:, t : t + 1], bias=pos[:, t : t + 1])
-                else:
-                    nc.vector.tensor_scalar(out=dst[:, t, :], in0=src[:, t, :], scalar1=neg[:, t : t + 1], scalar2=pos[:, t : t + 1], op0=ALU.mult, op1=ALU.add)
+                nc.scalar.activation(out=hidden[ci][:, t, :], in_=banks[t][:], func=ACT.Tanh)
 
-        def residual(ci, c0, n, u0, lin):
-            usq = tile("usq%d" % ci, [P, n], F32)
-            cub = tile("cub%d" % ci, [P, n], F32)
-            res = tile("res%d" % ci, [P, n], F32)
-            nc.scalar.activation(out=usq[:], in_=u0, func=ACT.Square)
-            nc.vector.scalar_tensor_tensor(out=cub[:], in0=usq[:], scalar=1.0, in1=u0, op0=ALU.subtract, op1=ALU.mult)
-            nc.vector.tensor_tensor(out=res[:], in0=cub[:], in1=lin, op=ALU.add)
-            nc.sync.dma_start(out=out[:, c0 : c0 + n], in_=res[:])
+        gather_pass1(0)
+        pre0 = first_layer_in_four_banks(0, 0)
+        gather_pass1(1)
+        pre1 = first_layer_in_four_banks(1, PACK)
+        gather_pass1(LAST)
+        tanh_of_four_banks(0, pre0)
+        pre_last = bank("pre_last", PACK - 1, [P, PACK, CHUNKS[LAST][1]])
+        for t in range(PACK):
+            for g in range(2):
+                first_product(pre_last[:, t, :], LAST, g, t)
 
-        head = CHUNKS[-1][0]
-        u0_head = bank("u0_head", "b0", [P, head])
-        lin_head = bank("lin_head", "b1", [P, head])
-        u0_last = bank("u0_last", "b2", [P, S - head])
-        lin_last = bank("lin_last", "b4", [P, S - head])
-        for ci, (c0, n, on_scalar) in enumerate(CHUNKS):
-            if ci > 0:
-                tanh(ci, zbanks[ci])
-            h = hs[ci]
-            sq = tile("sq%d" % ci, [P, PACK, n], F32)
-            mc = tile("mc%d" % ci, [P, PACK, n], F32)
-            ma = tile("ma%d" % ci, [P, PACK, n], F32)
-            zu0 = tile("zu0_%d" % ci, [P, n, PACK], BF16)
-            zd = tile("zd_%d" % ci, [P, 2, n, PACK], BF16)
-            u0 = u0_head[:, c0 : c0 + n] if c0 < head else u0_last[:]
-            lin = lin_head[:, c0 : c0 + n] if c0 < head else lin_last[:]
-            nc.scalar.activation(out=sq[:], in_=h[:], func=ACT.Square)
-            affine(mc, sq, c_neg, c_pos, on_scalar)
-            nc.vector.tensor_tensor(
-                out=walk_dst(zu0[:]), in0=walk_src(h),
-                in1=unit_sb[:].unsqueeze(1).unsqueeze(3).to_broadcast([P, n // 4, PACK, 4]), op=ALU.mult,
+        w2_rounded = tile("w2_rounded", [P, N, PACK], BF16)
+        nc.vector.tensor_copy(out=into_words(w2_rounded[:]), in_=by_runs(w2_raw[:]))
+        w2_words, w2_scales = quantise("w2", w2_rounded[:].rearrange("p n j -> p (n j)"), N)
+
+        factors = tile("factors", [P, 4, PACK], F32)
+        a_pos, c_pos, a_neg, c_neg = [factors[:, i, :] for i in range(4)]
+        unit_twice = unit_sb[:].unsqueeze(1).to_broadcast([P, 2, PACK])
+        nc.vector.tensor_tensor(out=slopes[:, 1, :], in0=wx_sb[:], in1=wx_sb[:], op=ALU.mult)
+        nc.vector.tensor_tensor(out=factors[:, 0:2, :], in0=slopes[:], in1=unit_twice, op=ALU.mult)
+        nc.vector.scalar_tensor_tensor(
+            out=factors[:, 2:4, :], in0=slopes[:], scalar=-1.0, in1=unit_twice, op0=ALU.mult, op1=ALU.mult
+        )
+
+        def second_product(dst, words, scales, start, stop):
+            nc.tensor.matmul_mx(
+                out=dst,
+                lhsT=w2_words[:].bitcast(FP8X4),
+                lhsT_scale=w2_scales[:],
+                rhs=words.bitcast(FP8X4),
+                rhs_scale=scales,
+                start=start,
+                stop=stop,
             )
-            affine(ma, sq, a_neg, a_pos, on_scalar)
+
+        def times_one_minus(dst, squares, neg, pos, on_vector):
+            for t in range(PACK):
+                scale, bias = neg[:, t : t + 1], pos[:, t : t + 1]
+                if on_vector:
+                    nc.vector.tensor_scalar(
+                        out=dst[:, t, :], in0=squares[:, t, :], scalar1=scale, scalar2=bias, op0=ALU.mult, op1=ALU.add
+                    )
+                else:
+                    nc.scalar.activation(
+                        out=dst[:, t, :], in_=squares[:, t, :], func=ACT.Identity, scale=scale, bias=bias
+                    )
+
+        def residual(name, c0, n, u0, linear):
+            u0_squared = tile(name + "_u0_squared", [P, n], F32)
+            cubic = tile(name + "_cubic", [P, n], F32)
+            result = tile(name + "_result", [P, n], F32)
+            nc.scalar.activation(out=u0_squared[:], in_=u0, func=ACT.Square)
+            nc.vector.scalar_tensor_tensor(
+                out=cubic[:], in0=u0_squared[:], scalar=1.0, in1=u0, op0=ALU.subtract, op1=ALU.mult
+            )
+            nc.vector.tensor_tensor(out=result[:], in0=cubic[:], in1=linear, op=ALU.add)
+            nc.sync.dma_start(out=out[:, c0 : c0 + n], in_=result[:])
+
+        head = CHUNKS[LAST][0]
+        u0_head = bank("u0_head", 0, [P, head])
+        linear_head = bank("linear_head", 1, [P, head])
+        u0_last = bank("u0_last", 2, [P, S - head])
+        linear_last = bank("linear_last", PACK, [P, S - head])
+        for ci, (c0, n) in enumerate(CHUNKS):
+            h = hidden[ci]
+            if ci == 1:
+                tanh_of_four_banks(ci, pre1)
+            if ci == LAST:
+                nc.scalar.activation(out=h[:], in_=pre_last[:], func=ACT.Tanh)
+            squares = tile("squares%d" % ci, [P, PACK, n], F32)
+            c_slope = tile("c_slope%d" % ci, [P, PACK, n], F32)
+            a_slope = tile("a_slope%d" % ci, [P, PACK, n], F32)
+            zu0 = tile("zu0_%d" % ci, [P, n, PACK], BF16)
+            z_linear = tile("z_linear%d" % ci, [P, 2, n, PACK], BF16)
+            u0 = u0_last[:] if ci == LAST else u0_head[:, c0 : c0 + n]
+            linear = linear_last[:] if ci == LAST else linear_head[:, c0 : c0 + n]
+            on_vector = ci == 0
+
+            nc.scalar.activation(out=squares[:], in_=h[:], func=ACT.Square)
+            times_one_minus(c_slope, squares, c_neg, c_pos, on_vector)
+            unit_by_runs = unit_sb[:].unsqueeze(1).unsqueeze(3).to_broadcast([P, n // RUN, PACK, RUN])
+            nc.vector.tensor_tensor(out=into_words(zu0[:]), in0=by_runs(h[:]), in1=unit_by_runs, op=ALU.mult)
+            times_one_minus(a_slope, squares, a_neg, a_pos, on_vector)
             words, scales = quantise("zu0_%d" % ci, zu0[:].rearrange("p n t -> p (n t)"), n)
-            mm2(u0, words[:], scales[:], True, True)
-            nc.vector.tensor_tensor(out=walk_dst(zd[:, 0]), in0=walk_src(mc), in1=walk_src(h), op=ALU.mult)
-            nc.vector.tensor_copy(out=walk_dst(zd[:, 1]), in_=walk_src(ma))
-            if ci < len(CHUNKS) - 1:
-                words, scales = quantise("zd_%d" % ci, zd[:].rearrange("p a n t -> p (a n t)"), 2 * n)
+            second_product(u0, words[:], scales[:], True, True)
+
+            nc.vector.tensor_tensor(
+                out=into_words(z_linear[:, 0]), in0=by_runs(c_slope[:]), in1=by_runs(h[:]), op=ALU.mult
+            )
+            nc.vector.tensor_copy(out=into_words(z_linear[:, 1]), in_=by_runs(a_slope[:]))
+            if ci == LAST:
                 for a in range(2):
-                    mm2(lin, words[:, a * n : (a + 1) * n], scales[:, a * n : (a + 1) * n], a == 0, a == 1)
+                    values = z_linear[:, a].rearrange("p n t -> p (n t)")
+                    words, scales = quantise("z_linear%d_%d" % (ci, a), values, n)
+                    second_product(linear, words[:], scales[:], a == 0, a == 1)
             else:
+                values = z_linear[:].rearrange("p a n t -> p (a n t)")
+                words, scales = quantise("z_linear%d" % ci, values, 2 * n)
                 for a in range(2):
-                    words, scales = quantise("zd_%d%d" % (ci, a), zd[:, a].rearrange("p n t -> p (n t)"), n)
-                    mm2(lin, words[:], scales[:], a == 0, a == 1)
-        residual(0, 0, head, u0_head[:], lin_head[:])
-        residual(1, head, S - head, u0_last[:], lin_last[:])
+                    cols = slice(a * n, (a + 1) * n)
+                    second_product(linear, words[:, cols], scales[:, cols], a == 0, a == 1)
+
+        residual("head", 0, head, u0_head[:], linear_head[:])
+        residual("last", head, S - head, u0_last[:], linear_last[:])

from contextlib import ExitStack

import concourse.mybir as mybir

K, T, S, H, N = 1024, 1024, 512, 512, 128
FLOPS = 2 * K * H * S + 3 * 2 * H * N * S

F32 = mybir.dt.float32
BF16 = mybir.dt.bfloat16
I32 = mybir.dt.int32
U32 = mybir.dt.uint32
U16 = mybir.dt.uint16
U8 = mybir.dt.uint8
FP8X4 = mybir.dt.float8_e4m3fn_x4
ACT = mybir.ActivationFunctionType
ALU = mybir.AluOpType

P = 128
PACK = 4
K_PASS = P * PACK
QUADRANTS, QUADRANT = 4, 32
LIST_ROWS = 16
RUN = 4
HALF = P // 2

M_VECTOR_PASS0 = 96
M_VECTOR_LAST = 48

CHUNKS = [(0, 128), (128, 256), (384, 128)]
LAST = len(CHUNKS) - 1


def tile_picked_ypinn_allen_p_kernel(
    tc, x_words, x_scales, w1, unit, wx, wt, w2, offs, out
):
    nc = tc.nc
    with ExitStack() as ctx:
        sb = ctx.enter_context(tc.tile_pool(name="sb", bufs=1))
        ps = ctx.enter_context(tc.psum_pool(name="ps", bufs=1))

        def tile(name, shape, dtype):
            return sb.tile(shape, dtype, name=name, align_bytes=64)

        def bank(name, index, shape):
            return ps.tile(shape, F32, name=name, tag="bank%d" % index)

        def quantise(name, values, columns):
            words = tile(name + "_words", [P, columns], U32)
            scales = tile(name + "_scales", [P, columns], U8)
            nc.vector.quantize_mx(out=words[:].bitcast(FP8X4), scales=scales[:], in_=values)
            return words, scales

        def by_runs(grouped):
            return grouped.rearrange("p t (c i) -> p c t i", i=RUN)

        def into_words(interleaved):
            return interleaved.rearrange("p (c i) t -> p c t i", i=RUN)

        offsets = tile("offsets", [P, S // LIST_ROWS], U16)
        x_word_table = [tile("x_word_table%d" % g, [P, T], U32) for g in range(2)]
        x_scale_table = tile("x_scale_table", [P, T], U8)
        w1_pass0 = tile("w1_pass0", [P, PACK, H], F32)
        w1_pass1 = [tile("w1_pass1_%d" % u, [P, PACK, H // 2], F32) for u in range(2)]
        w2_raw = tile("w2_raw", [P, PACK, N], F32)
        unit_sb = tile("unit_sb", [P, PACK], F32)
        wx_sb = tile("wx_sb", [P, PACK], F32)
        slopes = tile("slopes", [P, 2, PACK], F32)

        def load_words(g):
            nc.sync.dma_start(
                out=x_word_table[g][:].bitcast(I32),
                in_=x_words[g].rearrange("p n t -> p (n t)").bitcast(I32),
            )

        def load_rows(dst, rows):
            nc.sync.dma_start(out=dst, in_=rows.rearrange("(p j) c -> p j c", j=PACK))

        nc.gpsimd.memset(x_scale_table[:].bitcast(I32), 0)
        load_words(0)
        nc.sync.dma_start(offsets[:], offs)
        for q in range(QUADRANTS):
            nc.sync.dma_start(
                out=x_scale_table[QUADRANT * q : QUADRANT * q + 8, :].bitcast(I32),
                in_=x_scales[:, 4 * q : 4 * q + 4, :].bitcast(I32),
            )
        load_rows(w1_pass0[:], w1[:K_PASS, :])
        for u in range(2):
            load_rows(w1_pass1[u][:], w1[K_PASS:, u * (H // 2) : (u + 1) * (H // 2)])
        load_words(1)
        load_rows(w2_raw[:], w2)
        for dst, src in ((unit_sb[:], unit), (wx_sb[:], wx), (slopes[:, 0, :], wt)):
            nc.sync.dma_start(out=dst, in_=src.rearrange("(p j) o -> p (j o)", j=PACK))

        picked_scales = tile("picked_scales", [P, S], U8)
        picked_words0 = tile("picked_words0", [P, S], U32)
        nc.vector.tensor_copy(out=picked_words0[:], in_=x_word_table[0][:].indirect(offsets[:]))
        nc.vector.tensor_copy(out=picked_scales[:], in_=x_scale_table[:].indirect(offsets[:]))

        w1_words, w1_scales = {}, {}

        def deal(raw):
            return raw[:].rearrange("p j (m t) -> p m j t", t=PACK)

        def quantise_w1(g, dealt):
            for u in range(2):
                values = dealt[:, 2 * u : 2 * u + 2].rearrange("p t m j -> p (t m j)")
                words, scales = quantise("w1_%d%d" % (g, u), values, 2 * P)
                for v in range(2):
                    w1_words[g, 2 * u + v] = words[:, v * P : (v + 1) * P]
                    w1_scales[g, 2 * u + v] = scales[:, v * P : (v + 1) * P]

        dealt0 = tile("w1_dealt0", [P, PACK, P, PACK], BF16)
        dst0 = dealt0[:].rearrange("p t m j -> p m j t")
        nc.vector.tensor_copy(out=dst0[:, :M_VECTOR_PASS0], in_=deal(w1_pass0)[:, :M_VECTOR_PASS0])
        nc.scalar.activation(out=dst0[:, M_VECTOR_PASS0:], in_=deal(w1_pass0)[:, M_VECTOR_PASS0:], func=ACT.Copy)
        quantise_w1(0, dealt0)

        dealt1 = tile("w1_dealt1", [P, PACK, P, PACK], BF16)
        dst1 = dealt1[:].rearrange("p t m j -> p m j t")
        split = HALF + M_VECTOR_LAST
        nc.scalar.activation(out=dst1[:, :HALF], in_=deal(w1_pass1[0]), func=ACT.Copy)
        nc.vector.tensor_copy(out=dst1[:, HALF:split], in_=deal(w1_pass1[1])[:, :M_VECTOR_LAST])
        nc.scalar.activation(out=dst1[:, split:], in_=deal(w1_pass1[1])[:, M_VECTOR_LAST:], func=ACT.Copy)
        quantise_w1(1, dealt1)

        picked_words1 = [tile("picked_words1_%d" % ci, [P, n], U32) for ci, (c0, n) in enumerate(CHUNKS)]
        hidden = [tile("hidden%d" % ci, [P, PACK, n], F32) for ci, (c0, n) in enumerate(CHUNKS)]

        def gather_pass1(ci):
            c0, n = CHUNKS[ci]
            entries = offsets[:, c0 // LIST_ROWS : (c0 + n) // LIST_ROWS]
            nc.vector.tensor_copy(out=picked_words1[ci][:], in_=x_word_table[1][:].indirect(entries))

        def first_product(dst, ci, g, t):
            c0, n = CHUNKS[ci]
            moving = picked_words0[:, c0 : c0 + n] if g == 0 else picked_words1[ci][:]
            nc.tensor.matmul_mx(
                out=dst,
                lhsT=w1_words[g, t].bitcast(FP8X4),
                lhsT_scale=w1_scales[g, t],
                rhs=moving.bitcast(FP8X4),
                rhs_scale=picked_scales[4 * g : P, c0 : c0 + n],
                start=(g == 0),
                stop=(g == 1),
            )

        def first_layer_in_four_banks(ci, first_bank):
            banks = [bank("pre%d_%d" % (ci, t), first_bank + t, [P, CHUNKS[ci][1]]) for t in range(PACK)]
            for g in range(2):
                for t in range(PACK):
                    first_product(banks[t][:], ci, g, t)
            return banks

        def tanh_of_four_banks(ci, banks):
            for t in range(PACK):
                nc.scalar.activation(out=hidden[ci][:, t, :], in_=banks[t][:], func=ACT.Tanh)

        gather_pass1(0)
        pre0 = first_layer_in_four_banks(0, 0)
        gather_pass1(1)
        pre1 = first_layer_in_four_banks(1, PACK)
        gather_pass1(LAST)
        tanh_of_four_banks(0, pre0)
        pre_last = bank("pre_last", PACK - 1, [P, PACK, CHUNKS[LAST][1]])
        for t in range(PACK):
            for g in range(2):
                first_product(pre_last[:, t, :], LAST, g, t)

        w2_rounded = tile("w2_rounded", [P, N, PACK], BF16)
        nc.vector.tensor_copy(out=into_words(w2_rounded[:]), in_=by_runs(w2_raw[:]))
        w2_words, w2_scales = quantise("w2", w2_rounded[:].rearrange("p n j -> p (n j)"), N)

        factors = tile("factors", [P, 4, PACK], F32)
        a_pos, c_pos, a_neg, c_neg = [factors[:, i, :] for i in range(4)]
        unit_twice = unit_sb[:].unsqueeze(1).to_broadcast([P, 2, PACK])
        nc.vector.tensor_tensor(out=slopes[:, 1, :], in0=wx_sb[:], in1=wx_sb[:], op=ALU.mult)
        nc.vector.tensor_tensor(out=factors[:, 0:2, :], in0=slopes[:], in1=unit_twice, op=ALU.mult)
        nc.vector.scalar_tensor_tensor(
            out=factors[:, 2:4, :], in0=slopes[:], scalar=-1.0, in1=unit_twice, op0=ALU.mult, op1=ALU.mult
        )

        def second_product(dst, words, scales, start, stop):
            nc.tensor.matmul_mx(
                out=dst,
                lhsT=w2_words[:].bitcast(FP8X4),
                lhsT_scale=w2_scales[:],
                rhs=words.bitcast(FP8X4),
                rhs_scale=scales,
                start=start,
                stop=stop,
            )

        def times_one_minus(dst, squares, neg, pos, on_vector):
            for t in range(PACK):
                scale, bias = neg[:, t : t + 1], pos[:, t : t + 1]
                if on_vector:
                    nc.vector.tensor_scalar(
                        out=dst[:, t, :], in0=squares[:, t, :], scalar1=scale, scalar2=bias, op0=ALU.mult, op1=ALU.add
                    )
                else:
                    nc.scalar.activation(
                        out=dst[:, t, :], in_=squares[:, t, :], func=ACT.Identity, scale=scale, bias=bias
                    )

        def residual(name, c0, n, u0, linear):
            u0_squared = tile(name + "_u0_squared", [P, n], F32)
            cubic = tile(name + "_cubic", [P, n], F32)
            result = tile(name + "_result", [P, n], F32)
            nc.scalar.activation(out=u0_squared[:], in_=u0, func=ACT.Square)
            nc.vector.scalar_tensor_tensor(
                out=cubic[:], in0=u0_squared[:], scalar=1.0, in1=u0, op0=ALU.subtract, op1=ALU.mult
            )
            nc.vector.tensor_tensor(out=result[:], in0=cubic[:], in1=linear, op=ALU.add)
            nc.sync.dma_start(out=out[:, c0 : c0 + n], in_=result[:])

        head = CHUNKS[LAST][0]
        u0_head = bank("u0_head", 0, [P, head])
        linear_head = bank("linear_head", 1, [P, head])
        u0_last = bank("u0_last", 2, [P, S - head])
        linear_last = bank("linear_last", PACK, [P, S - head])
        for ci, (c0, n) in enumerate(CHUNKS):
            h = hidden[ci]
            if ci == 1:
                tanh_of_four_banks(ci, pre1)
            if ci == LAST:
                nc.scalar.activation(out=h[:], in_=pre_last[:], func=ACT.Tanh)
            squares = tile("squares%d" % ci, [P, PACK, n], F32)
            c_slope = tile("c_slope%d" % ci, [P, PACK, n], F32)
            a_slope = tile("a_slope%d" % ci, [P, PACK, n], F32)
            zu0 = tile("zu0_%d" % ci, [P, n, PACK], BF16)
            z_linear = tile("z_linear%d" % ci, [P, 2, n, PACK], BF16)
            u0 = u0_last[:] if ci == LAST else u0_head[:, c0 : c0 + n]
            linear = linear_last[:] if ci == LAST else linear_head[:, c0 : c0 + n]
            on_vector = ci == 0

            nc.scalar.activation(out=squares[:], in_=h[:], func=ACT.Square)
            times_one_minus(c_slope, squares, c_neg, c_pos, on_vector)
            unit_by_runs = unit_sb[:].unsqueeze(1).unsqueeze(3).to_broadcast([P, n // RUN, PACK, RUN])
            nc.vector.tensor_tensor(out=into_words(zu0[:]), in0=by_runs(h[:]), in1=unit_by_runs, op=ALU.mult)
            times_one_minus(a_slope, squares, a_neg, a_pos, on_vector)
            words, scales = quantise("zu0_%d" % ci, zu0[:].rearrange("p n t -> p (n t)"), n)
            second_product(u0, words[:], scales[:], True, True)

            nc.vector.tensor_tensor(
                out=into_words(z_linear[:, 0]), in0=by_runs(c_slope[:]), in1=by_runs(h[:]), op=ALU.mult
            )
            nc.vector.tensor_copy(out=into_words(z_linear[:, 1]), in_=by_runs(a_slope[:]))
            if ci == LAST:
                for a in range(2):
                    values = z_linear[:, a].rearrange("p n t -> p (n t)")
                    words, scales = quantise("z_linear%d_%d" % (ci, a), values, n)
                    second_product(linear, words[:], scales[:], a == 0, a == 1)
            else:
                values = z_linear[:].rearrange("p a n t -> p (a n t)")
                words, scales = quantise("z_linear%d" % ci, values, 2 * n)
                for a in range(2):
                    cols = slice(a * n, (a + 1) * n)
                    second_product(linear, words[:, cols], scales[:, cols], a == 0, a == 1)

        residual("head", 0, head, u0_head[:], linear_head[:])
        residual("last", head, S - head, u0_last[:], linear_last[:])
